import numpy as np
CORES = [32,33,34,35,288,289,290,291]
N = 8
def setup_inputs(rng):
    return {"x": rng.standard_normal((N, 128, 512), dtype=np.float32)}
def reference(x):
    s = x.sum(axis=0, dtype=np.float64).astype(x.dtype)
    s = np.maximum(s, 0)
    return {"y": np.broadcast_to(s, (N,) + s.shape)}

@@ -1,0 +1,91 @@
+from concourse.bass import DstId, RemoteDMATransfer
+
+NP = 8
+PW = 64
+
+SCRATCH = {
+    "xs":   ("dram", [NP, 128, PW], "float32"),
+    "land": ("dram", [4, 128, PW], "float32"),
+    "hs":   ("dram", [2, 128, PW], "float32"),
+    "zd":   ("dram", [128, PW], "float32"),
+    "zs":   ("sbuf", [128, PW], "float32"),
+    "fin":  ("dram", [NP, 128, PW], "float32"),
+}
+SEMAPHORES = ["ld", "rsarr", "rlarr", "harr", "farr", "sent", "zm", "zr", "st"]
+
+
+def rank_program(g, core, T, topo):
+    base_a = T.cores[0] - T.cores[0] % 8
+    base_b = T.cores[4] - T.cores[4] % 8
+    off = base_a % 128
+    relay_even = 3 * 128 + off
+    relay_odd = 1 * 128 + off
+
+    def relay_of(p):
+        return (relay_even if p % 2 == 0 else relay_odd) + p
+
+    def did(dst):
+        rid, pid = topo.addr(dst, core)
+        return DstId(rid=rid, pnc=pid)
+
+    base = core - core % 8
+    i = core % 8
+    sem = T.sem
+
+    if base in (relay_even, relay_odd):
+        if relay_of(i) != core:
+            return
+        g.wait_ge(sem.rlarr, 16)
+        helpers = [base_a + 4 + i // 2, base_b + 4 + i // 2]
+        g.remote_dma_fused([RemoteDMATransfer(
+            dst_ids=[did(h) for h in helpers], dma_engine_mask=0x00FF, remote_sem=sem.harr,
+            srcs=[T.land[0], T.land[1]], dsts=[T.hs[i % 2], T.hs[i % 2]], alu_op=1)], local_sem=sem.sent)
+        g.wait_ge(sem.sent, 8)
+        return
+
+    if base not in (base_a, base_b):
+        return
+    side = 0 if base == base_a else 1
+    is_rank = i < 4
+
+    if is_rank:
+        g.sync.dma_start(T.xs[:], T.x[:]).then_inc(sem.ld, 16)
+        g.wait_ge(sem.ld, 16)
+        trs = []
+        for k, p in enumerate([q for q in range(NP) if q != i]):
+            trs.append(RemoteDMATransfer(
+                dst_ids=[did(base + p)], dma_engine_mask=0b11 << (2 * k), remote_sem=sem.rsarr,
+                srcs=[T.xs[p]], dsts=[T.land[i]], alu_op=0))
+        g.remote_dma_fused(trs, local_sem=sem.sent)
+    else:
+        g.vector.memset(T.zs[:], 0.0).then_inc(sem.zm, 1)
+        g.sync.wait_ge(sem.zm, 1)
+        g.sync.dma_start(T.zd[:], T.zs[:]).then_inc(sem.zr, 16)
+
+    if is_rank:
+        g.wait_ge(sem.rsarr, 3 * 2)
+        srcs = [T.xs[i] if r == i else T.land[r] for r in range(4)]
+    else:
+        g.wait_ge(sem.rsarr, 4 * 2)
+        srcs = [T.land[r] for r in range(4)]
+    g.remote_dma_fused([RemoteDMATransfer(
+        dst_ids=[did(relay_of(i))], dma_engine_mask=0x00FF, remote_sem=sem.rlarr,
+        srcs=srcs, dsts=[T.land[side]], alu_op=1)], local_sem=sem.sent)
+
+    if is_rank:
+        g.sync.wait_ge(sem.farr, NP * 8)
+        g.sync.dma_start(T.y[:], T.fin[:]).then_inc(sem.st, 16)
+        g.sync.wait_ge(sem.st, 16)
+        g.wait_ge(sem.sent, 7 * 2 + 8)
+    else:
+        j = i - 4
+        g.wait_ge(sem.zr, 16)
+        g.wait_ge(sem.harr, 16)
+        ranks = [base + r for r in range(4)]
+        trs = []
+        for h in range(2):
+            trs.append(RemoteDMATransfer(
+                dst_ids=[did(r) for r in ranks], dma_engine_mask=0x00FF << (8 * h), remote_sem=sem.farr,
+                srcs=[T.hs[h], T.zd[:]], dsts=[T.fin[2 * j + h]] * 4, alu_op=2))
+        g.remote_dma_fused(trs, local_sem=sem.sent)
+        g.wait_ge(sem.sent, 8 + 16)

@@ -11,7 +11,7 @@ SCRATCH = {
     "zs":   ("sbuf", [128, PW], "float32"),
     "fin":  ("dram", [NP, 128, PW], "float32"),
 }
-SEMAPHORES = ["ld", "rsarr", "rlarr", "harr", "farr", "sent", "zm", "zr", "st"]
+SEMAPHORES = ["ld0", "ld1", "rsarr", "rlarr", "harr0", "harr1", "farr0", "farr1", "sent", "zm", "zr", "st0", "st1"]
 
 
 def rank_program(g, core, T, topo):
@@ -35,57 +35,57 @@ def rank_program(g, core, T, topo):
     if base in (relay_even, relay_odd):
         if relay_of(i) != core:
             return
+        wave = 0 if i >= 4 else 1
         g.wait_ge(sem.rlarr, 16)
-        helpers = [base_a + 4 + i // 2, base_b + 4 + i // 2]
+        helpers = [base_a + 4 + i % 4, base_b + 4 + i % 4]
         g.remote_dma_fused([RemoteDMATransfer(
-            dst_ids=[did(h) for h in helpers], dma_engine_mask=0x00FF, remote_sem=sem.harr,
-            srcs=[T.land[0], T.land[1]], dsts=[T.hs[i % 2], T.hs[i % 2]], alu_op=1)], local_sem=sem.sent)
+            dst_ids=[did(h) for h in helpers], dma_engine_mask=0x00FF, remote_sem=(sem.harr0, sem.harr1)[wave],
+            srcs=[T.land[0], T.land[1]], dsts=[T.hs[wave], T.hs[wave]], alu_op=1)], local_sem=sem.sent)
         g.wait_ge(sem.sent, 8)
         return
 
     if base not in (base_a, base_b):
         return
     side = 0 if base == base_a else 1
-    is_rank = i < 4
 
-    if is_rank:
-        g.sync.dma_start(T.xs[:], T.x[:]).then_inc(sem.ld, 16)
-        g.wait_ge(sem.ld, 16)
-        trs = []
-        for k, p in enumerate([q for q in range(NP) if q != i]):
-            trs.append(RemoteDMATransfer(
-                dst_ids=[did(base + p)], dma_engine_mask=0b11 << (2 * k), remote_sem=sem.rsarr,
-                srcs=[T.xs[p]], dsts=[T.land[i]], alu_op=0))
-        g.remote_dma_fused(trs, local_sem=sem.sent)
+    def w2(srcs):
+        g.remote_dma_fused([RemoteDMATransfer(
+            dst_ids=[did(relay_of(i))], dma_engine_mask=0x00FF, remote_sem=sem.rlarr,
+            srcs=srcs, dsts=[T.land[side]], alu_op=1)], local_sem=sem.sent)
+
+    if i < 4:
+        g.sync.dma_start(T.xs[4:8], T.x[64:128, :]).then_inc(sem.ld0, 16)
+        g.scalar.dma_start(T.xs[0:4], T.x[0:64, :]).then_inc(sem.ld1, 16)
+
+        def w1(pieces):
+            g.remote_dma_fused([RemoteDMATransfer(
+                dst_ids=[did(base + p)], dma_engine_mask=0xF << (4 * k), remote_sem=sem.rsarr,
+                srcs=[T.xs[p]], dsts=[T.land[i]], alu_op=0) for k, p in enumerate(pieces)], local_sem=sem.sent)
+
+        g.wait_ge(sem.ld0, 16)
+        w1([4, 5, 6, 7])
+        g.wait_ge(sem.ld1, 16)
+        w1([p for p in range(4) if p != i])
+        g.wait_ge(sem.rsarr, 3 * 4)
+        w2([T.xs[i] if r == i else T.land[r] for r in range(4)])
+        g.scalar.wait_ge(sem.farr0, 64)
+        g.scalar.dma_start(T.y[64:128, :], T.fin[4:8]).then_inc(sem.st0, 16)
+        g.sync.wait_ge(sem.farr1, 64)
+        g.sync.dma_start(T.y[0:64, :], T.fin[0:4]).then_inc(sem.st1, 16)
+        g.scalar.wait_ge(sem.st0, 16)
+        g.sync.wait_ge(sem.st1, 16)
+        g.wait_ge(sem.sent, 16 + 12 + 8)
     else:
         g.vector.memset(T.zs[:], 0.0).then_inc(sem.zm, 1)
         g.sync.wait_ge(sem.zm, 1)
         g.sync.dma_start(T.zd[:], T.zs[:]).then_inc(sem.zr, 16)
-
-    if is_rank:
-        g.wait_ge(sem.rsarr, 3 * 2)
-        srcs = [T.xs[i] if r == i else T.land[r] for r in range(4)]
-    else:
-        g.wait_ge(sem.rsarr, 4 * 2)
-        srcs = [T.land[r] for r in range(4)]
-    g.remote_dma_fused([RemoteDMATransfer(
-        dst_ids=[did(relay_of(i))], dma_engine_mask=0x00FF, remote_sem=sem.rlarr,
-        srcs=srcs, dsts=[T.land[side]], alu_op=1)], local_sem=sem.sent)
-
-    if is_rank:
-        g.sync.wait_ge(sem.farr, NP * 8)
-        g.sync.dma_start(T.y[:], T.fin[:]).then_inc(sem.st, 16)
-        g.sync.wait_ge(sem.st, 16)
-        g.wait_ge(sem.sent, 7 * 2 + 8)
-    else:
-        j = i - 4
+        g.wait_ge(sem.rsarr, 4 * 4)
+        w2([T.land[r] for r in range(4)])
         g.wait_ge(sem.zr, 16)
-        g.wait_ge(sem.harr, 16)
         ranks = [base + r for r in range(4)]
-        trs = []
-        for h in range(2):
-            trs.append(RemoteDMATransfer(
-                dst_ids=[did(r) for r in ranks], dma_engine_mask=0x00FF << (8 * h), remote_sem=sem.farr,
-                srcs=[T.hs[h], T.zd[:]], dsts=[T.fin[2 * j + h]] * 4, alu_op=2))
-        g.remote_dma_fused(trs, local_sem=sem.sent)
-        g.wait_ge(sem.sent, 8 + 16)
+        for wave in range(2):
+            g.wait_ge((sem.harr0, sem.harr1)[wave], 8)
+            g.remote_dma_fused([RemoteDMATransfer(
+                dst_ids=[did(r) for r in ranks], dma_engine_mask=0xFFFF, remote_sem=(sem.farr0, sem.farr1)[wave],
+                srcs=[T.hs[wave], T.zd[:]], dsts=[T.fin[i if wave == 0 else i - 4]] * 4, alu_op=2)], local_sem=sem.sent)
+        g.wait_ge(sem.sent, 8 + 32)

@@ -1,17 +1,17 @@
 from concourse.bass import DstId, RemoteDMATransfer
 
-NP = 8
-PW = 64
+NP = 16
+PW = 32
 
 SCRATCH = {
     "xs":   ("dram", [NP, 128, PW], "float32"),
-    "land": ("dram", [4, 128, PW], "float32"),
-    "hs":   ("dram", [2, 128, PW], "float32"),
+    "land": ("dram", [8, 128, PW], "float32"),
+    "hs":   ("dram", [4, 128, PW], "float32"),
     "zd":   ("dram", [128, PW], "float32"),
     "zs":   ("sbuf", [128, PW], "float32"),
     "fin":  ("dram", [NP, 128, PW], "float32"),
 }
-SEMAPHORES = ["ld0", "ld1", "rsarr", "rlarr", "harr0", "harr1", "farr0", "farr1", "sent", "zm", "zr", "st0", "st1"]
+SEMAPHORES = ["ld0", "ld1", "rs0", "rs1", "rlarr", "harr0", "harr1", "farr0", "farr1", "sent", "zm", "zr", "st0", "st1"]
 
 
 def rank_program(g, core, T, topo):
@@ -22,7 +22,8 @@ def rank_program(g, core, T, topo):
     relay_odd = 1 * 128 + off
 
     def relay_of(p):
-        return (relay_even if p % 2 == 0 else relay_odd) + p
+        k = p % 8
+        return (relay_even if k % 2 == 0 else relay_odd) + (k // 2) * 2 + p // 8
 
     def did(dst):
         rid, pid = topo.addr(dst, core)
@@ -31,61 +32,66 @@ def rank_program(g, core, T, topo):
     base = core - core % 8
     i = core % 8
     sem = T.sem
+    ld, rs = (sem.ld0, sem.ld1), (sem.rs0, sem.rs1)
+    harr, farr = (sem.harr0, sem.harr1), (sem.farr0, sem.farr1)
 
     if base in (relay_even, relay_odd):
-        if relay_of(i) != core:
-            return
-        wave = 0 if i >= 4 else 1
+        par = 0 if base == relay_even else 1
+        wave = 1 - i % 2
         g.wait_ge(sem.rlarr, 16)
-        helpers = [base_a + 4 + i % 4, base_b + 4 + i % 4]
+        helpers = [base_a + 4 + i // 2, base_b + 4 + i // 2]
         g.remote_dma_fused([RemoteDMATransfer(
-            dst_ids=[did(h) for h in helpers], dma_engine_mask=0x00FF, remote_sem=(sem.harr0, sem.harr1)[wave],
-            srcs=[T.land[0], T.land[1]], dsts=[T.hs[wave], T.hs[wave]], alu_op=1)], local_sem=sem.sent)
+            dst_ids=[did(h) for h in helpers], dma_engine_mask=0x00FF, remote_sem=harr[wave],
+            srcs=[T.land[0], T.land[1]], dsts=[T.hs[2 * wave + par]] * 2, alu_op=1)], local_sem=sem.sent)
         g.wait_ge(sem.sent, 8)
         return
 
     if base not in (base_a, base_b):
         return
     side = 0 if base == base_a else 1
+    is_rank = i < 4
 
-    def w2(srcs):
+    def w2(wave):
+        p = 8 * (1 - wave) + i
+        g.wait_ge(rs[wave], 6 if is_rank else 8)
         g.remote_dma_fused([RemoteDMATransfer(
-            dst_ids=[did(relay_of(i))], dma_engine_mask=0x00FF, remote_sem=sem.rlarr,
-            srcs=srcs, dsts=[T.land[side]], alu_op=1)], local_sem=sem.sent)
+            dst_ids=[did(relay_of(p))], dma_engine_mask=0x00FF, remote_sem=sem.rlarr,
+            srcs=[T.xs[p] if r == i else T.land[4 * wave + r] for r in range(4)],
+            dsts=[T.land[side]], alu_op=1)], local_sem=sem.sent)
 
-    if i < 4:
-        g.sync.dma_start(T.xs[4:8], T.x[64:128, :]).then_inc(sem.ld0, 16)
-        g.scalar.dma_start(T.xs[0:4], T.x[0:64, :]).then_inc(sem.ld1, 16)
-
-        def w1(pieces):
+    if is_rank:
+        g.sync.dma_start(T.xs[8:16], T.x[64:128, :]).then_inc(sem.ld0, 16)
+        g.scalar.dma_start(T.xs[0:8], T.x[0:64, :]).then_inc(sem.ld1, 16)
+        for wave in range(2):
+            g.wait_ge(ld[wave], 16)
+            first = 8 * (1 - wave)
             g.remote_dma_fused([RemoteDMATransfer(
-                dst_ids=[did(base + p)], dma_engine_mask=0xF << (4 * k), remote_sem=sem.rsarr,
-                srcs=[T.xs[p]], dsts=[T.land[i]], alu_op=0) for k, p in enumerate(pieces)], local_sem=sem.sent)
-
-        g.wait_ge(sem.ld0, 16)
-        w1([4, 5, 6, 7])
-        g.wait_ge(sem.ld1, 16)
-        w1([p for p in range(4) if p != i])
-        g.wait_ge(sem.rsarr, 3 * 4)
-        w2([T.xs[i] if r == i else T.land[r] for r in range(4)])
+                dst_ids=[did(base + k)], dma_engine_mask=0b11 << (2 * n), remote_sem=rs[wave],
+                srcs=[T.xs[first + k]], dsts=[T.land[4 * wave + i]], alu_op=0)
+                for n, k in enumerate([q for q in range(8) if q != i])], local_sem=sem.sent)
+        w2(0)
+        w2(1)
         g.scalar.wait_ge(sem.farr0, 64)
-        g.scalar.dma_start(T.y[64:128, :], T.fin[4:8]).then_inc(sem.st0, 16)
+        g.scalar.dma_start(T.y[64:128, :], T.fin[8:16]).then_inc(sem.st0, 16)
         g.sync.wait_ge(sem.farr1, 64)
-        g.sync.dma_start(T.y[0:64, :], T.fin[0:4]).then_inc(sem.st1, 16)
+        g.sync.dma_start(T.y[0:64, :], T.fin[0:8]).then_inc(sem.st1, 16)
         g.scalar.wait_ge(sem.st0, 16)
         g.sync.wait_ge(sem.st1, 16)
-        g.wait_ge(sem.sent, 16 + 12 + 8)
+        g.wait_ge(sem.sent, 28 + 16)
     else:
+        j = i - 4
         g.vector.memset(T.zs[:], 0.0).then_inc(sem.zm, 1)
         g.sync.wait_ge(sem.zm, 1)
         g.sync.dma_start(T.zd[:], T.zs[:]).then_inc(sem.zr, 16)
-        g.wait_ge(sem.rsarr, 4 * 4)
-        w2([T.land[r] for r in range(4)])
+        w2(0)
+        w2(1)
         g.wait_ge(sem.zr, 16)
         ranks = [base + r for r in range(4)]
         for wave in range(2):
-            g.wait_ge((sem.harr0, sem.harr1)[wave], 8)
+            g.wait_ge(harr[wave], 16)
+            first = 8 * (1 - wave)
             g.remote_dma_fused([RemoteDMATransfer(
-                dst_ids=[did(r) for r in ranks], dma_engine_mask=0xFFFF, remote_sem=(sem.farr0, sem.farr1)[wave],
-                srcs=[T.hs[wave], T.zd[:]], dsts=[T.fin[i if wave == 0 else i - 4]] * 4, alu_op=2)], local_sem=sem.sent)
-        g.wait_ge(sem.sent, 8 + 32)
+                dst_ids=[did(r) for r in ranks], dma_engine_mask=0xFF << (8 * h), remote_sem=farr[wave],
+                srcs=[T.hs[2 * wave + h], T.zd[:]], dsts=[T.fin[first + 2 * j + h]] * 4, alu_op=2) for h in range(2)],
+                local_sem=sem.sent)
+        g.wait_ge(sem.sent, 16 + 32)

@@ -1,17 +1,22 @@
 from concourse.bass import DstId, RemoteDMATransfer
 
-NP = 16
-PW = 32
+NW = 2
+WPC = NW // 2
+W1E = 2 // WPC
+NP = 8 * NW
+PW = 512 // NP
+XR = 128 // NW
 
 SCRATCH = {
     "xs":   ("dram", [NP, 128, PW], "float32"),
-    "land": ("dram", [8, 128, PW], "float32"),
-    "hs":   ("dram", [4, 128, PW], "float32"),
+    "land": ("dram", [4 * NW, 128, PW], "float32"),
+    "hs":   ("dram", [2 * NW, 128, PW], "float32"),
     "zd":   ("dram", [128, PW], "float32"),
     "zs":   ("sbuf", [128, PW], "float32"),
     "fin":  ("dram", [NP, 128, PW], "float32"),
 }
-SEMAPHORES = ["ld0", "ld1", "rs0", "rs1", "rlarr", "harr0", "harr1", "farr0", "farr1", "sent", "zm", "zr", "st0", "st1"]
+SEMAPHORES = (["ld0", "ld1", "sent", "zm", "zr"] + ["rl%d" % c for c in range(NW // 2)]
+              + ["%s%d" % (n, w) for n in ("rs", "harr", "farr", "st") for w in range(NW)])
 
 
 def rank_program(g, core, T, topo):
@@ -21,9 +26,8 @@ def rank_program(g, core, T, topo):
     relay_even = 3 * 128 + off
     relay_odd = 1 * 128 + off
 
-    def relay_of(p):
-        k = p % 8
-        return (relay_even if k % 2 == 0 else relay_odd) + (k // 2) * 2 + p // 8
+    def relay_of(w, k):
+        return (relay_even if k % 2 == 0 else relay_odd) + (k // 2) * 2 + w % 2
 
     def did(dst):
         rid, pid = topo.addr(dst, core)
@@ -32,18 +36,17 @@ def rank_program(g, core, T, topo):
     base = core - core % 8
     i = core % 8
     sem = T.sem
-    ld, rs = (sem.ld0, sem.ld1), (sem.rs0, sem.rs1)
-    harr, farr = (sem.harr0, sem.harr1), (sem.farr0, sem.farr1)
 
     if base in (relay_even, relay_odd):
         par = 0 if base == relay_even else 1
-        wave = 1 - i % 2
-        g.wait_ge(sem.rlarr, 16)
         helpers = [base_a + 4 + i // 2, base_b + 4 + i // 2]
-        g.remote_dma_fused([RemoteDMATransfer(
-            dst_ids=[did(h) for h in helpers], dma_engine_mask=0x00FF, remote_sem=harr[wave],
-            srcs=[T.land[0], T.land[1]], dsts=[T.hs[2 * wave + par]] * 2, alu_op=1)], local_sem=sem.sent)
-        g.wait_ge(sem.sent, 8)
+        for c in range(NW // 2):
+            w = 2 * c + i % 2
+            g.wait_ge(sem["rl%d" % c], 16)
+            g.remote_dma_fused([RemoteDMATransfer(
+                dst_ids=[did(h) for h in helpers], dma_engine_mask=0x00FF, remote_sem=sem["harr%d" % w],
+                srcs=[T.land[2 * c], T.land[2 * c + 1]], dsts=[T.hs[2 * w + par]] * 2, alu_op=1)], local_sem=sem.sent)
+        g.wait_ge(sem.sent, 8 * (NW // 2))
         return
 
     if base not in (base_a, base_b):
@@ -51,47 +54,47 @@ def rank_program(g, core, T, topo):
     side = 0 if base == base_a else 1
     is_rank = i < 4
 
-    def w2(wave):
-        p = 8 * (1 - wave) + i
-        g.wait_ge(rs[wave], 6 if is_rank else 8)
+    def w2(w):
+        g.wait_ge(sem["rs%d" % w], (3 if is_rank else 4) * W1E)
         g.remote_dma_fused([RemoteDMATransfer(
-            dst_ids=[did(relay_of(p))], dma_engine_mask=0x00FF, remote_sem=sem.rlarr,
-            srcs=[T.xs[p] if r == i else T.land[4 * wave + r] for r in range(4)],
-            dsts=[T.land[side]], alu_op=1)], local_sem=sem.sent)
+            dst_ids=[did(relay_of(w, i))], dma_engine_mask=0x00FF, remote_sem=sem["rl%d" % (w // 2)],
+            srcs=[T.xs[8 * w + i] if r == i else T.land[4 * w + r] for r in range(4)],
+            dsts=[T.land[2 * (w // 2) + side]], alu_op=1)], local_sem=sem.sent)
 
     if is_rank:
-        g.sync.dma_start(T.xs[8:16], T.x[64:128, :]).then_inc(sem.ld0, 16)
-        g.scalar.dma_start(T.xs[0:8], T.x[0:64, :]).then_inc(sem.ld1, 16)
-        for wave in range(2):
-            g.wait_ge(ld[wave], 16)
-            first = 8 * (1 - wave)
+        g.sync.dma_start(T.xs[0:NP // 2], T.x[0:64, :]).then_inc(sem.ld0, 16)
+        g.scalar.dma_start(T.xs[NP // 2:NP], T.x[64:128, :]).then_inc(sem.ld1, 16)
+        emask = (1 << W1E) - 1
+        for c in range(2):
+            g.wait_ge((sem.ld0, sem.ld1)[c], 16)
+            todo = [(w, k) for w in range(WPC * c, WPC * (c + 1)) for k in range(8) if k != i]
             g.remote_dma_fused([RemoteDMATransfer(
-                dst_ids=[did(base + k)], dma_engine_mask=0b11 << (2 * n), remote_sem=rs[wave],
-                srcs=[T.xs[first + k]], dsts=[T.land[4 * wave + i]], alu_op=0)
-                for n, k in enumerate([q for q in range(8) if q != i])], local_sem=sem.sent)
-        w2(0)
-        w2(1)
-        g.scalar.wait_ge(sem.farr0, 64)
-        g.scalar.dma_start(T.y[64:128, :], T.fin[8:16]).then_inc(sem.st0, 16)
-        g.sync.wait_ge(sem.farr1, 64)
-        g.sync.dma_start(T.y[0:64, :], T.fin[0:8]).then_inc(sem.st1, 16)
-        g.scalar.wait_ge(sem.st0, 16)
-        g.sync.wait_ge(sem.st1, 16)
-        g.wait_ge(sem.sent, 28 + 16)
+                dst_ids=[did(base + k)], dma_engine_mask=emask << (W1E * n), remote_sem=sem["rs%d" % w],
+                srcs=[T.xs[8 * w + k]], dsts=[T.land[4 * w + i]], alu_op=0)
+                for n, (w, k) in enumerate(todo)], local_sem=sem.sent)
+        for w in range(NW):
+            w2(w)
+        for w in range(NW):
+            q = g.sync if w % 2 == 0 else g.scalar
+            q.wait_ge(sem["farr%d" % w], 64)
+            q.dma_start(T.y[XR * w:XR * (w + 1), :], T.fin[8 * w:8 * (w + 1)]).then_inc(sem["st%d" % w], 16)
+        for w in range(NW):
+            q = g.sync if w % 2 == 0 else g.scalar
+            q.wait_ge(sem["st%d" % w], 16)
+        g.wait_ge(sem.sent, (7 * W1E + 8) * NW)
     else:
         j = i - 4
         g.vector.memset(T.zs[:], 0.0).then_inc(sem.zm, 1)
         g.sync.wait_ge(sem.zm, 1)
         g.sync.dma_start(T.zd[:], T.zs[:]).then_inc(sem.zr, 16)
-        w2(0)
-        w2(1)
+        for w in range(NW):
+            w2(w)
         g.wait_ge(sem.zr, 16)
         ranks = [base + r for r in range(4)]
-        for wave in range(2):
-            g.wait_ge(harr[wave], 16)
-            first = 8 * (1 - wave)
+        for w in range(NW):
+            g.wait_ge(sem["harr%d" % w], 16)
             g.remote_dma_fused([RemoteDMATransfer(
-                dst_ids=[did(r) for r in ranks], dma_engine_mask=0xFF << (8 * h), remote_sem=farr[wave],
-                srcs=[T.hs[2 * wave + h], T.zd[:]], dsts=[T.fin[first + 2 * j + h]] * 4, alu_op=2) for h in range(2)],
+                dst_ids=[did(r) for r in ranks], dma_engine_mask=0xFF << (8 * h), remote_sem=sem["farr%d" % w],
+                srcs=[T.hs[2 * w + h], T.zd[:]], dsts=[T.fin[8 * w + 2 * j + h]] * 4, alu_op=2) for h in range(2)],
                 local_sem=sem.sent)
-        g.wait_ge(sem.sent, 16 + 32)
+        g.wait_ge(sem.sent, (8 + 16) * NW)

from concourse.bass import DstId, RemoteDMATransfer

NW = 2
WPC = NW // 2
W1E = 2 // WPC
NP = 8 * NW
PW = 512 // NP
XR = 128 // NW

SCRATCH = {
    "xs":   ("dram", [NP, 128, PW], "float32"),
    "land": ("dram", [4 * NW, 128, PW], "float32"),
    "hs":   ("dram", [2 * NW, 128, PW], "float32"),
    "zd":   ("dram", [128, PW], "float32"),
    "zs":   ("sbuf", [128, PW], "float32"),
    "fin":  ("dram", [NP, 128, PW], "float32"),
}
SEMAPHORES = (["ld0", "ld1", "sent", "zm", "zr"] + ["rl%d" % c for c in range(NW // 2)]
              + ["%s%d" % (n, w) for n in ("rs", "harr", "farr", "st") for w in range(NW)])


def rank_program(g, core, T, topo):
    base_a = T.cores[0] - T.cores[0] % 8
    base_b = T.cores[4] - T.cores[4] % 8
    off = base_a % 128
    relay_even = 3 * 128 + off
    relay_odd = 1 * 128 + off

    def relay_of(w, k):
        return (relay_even if k % 2 == 0 else relay_odd) + (k // 2) * 2 + w % 2

    def did(dst):
        rid, pid = topo.addr(dst, core)
        return DstId(rid=rid, pnc=pid)

    base = core - core % 8
    i = core % 8
    sem = T.sem

    if base in (relay_even, relay_odd):
        par = 0 if base == relay_even else 1
        helpers = [base_a + 4 + i // 2, base_b + 4 + i // 2]
        for c in range(NW // 2):
            w = 2 * c + i % 2
            g.wait_ge(sem["rl%d" % c], 16)
            g.remote_dma_fused([RemoteDMATransfer(
                dst_ids=[did(h) for h in helpers], dma_engine_mask=0x00FF, remote_sem=sem["harr%d" % w],
                srcs=[T.land[2 * c], T.land[2 * c + 1]], dsts=[T.hs[2 * w + par]] * 2, alu_op=1)], local_sem=sem.sent)
        g.wait_ge(sem.sent, 8 * (NW // 2))
        return

    if base not in (base_a, base_b):
        return
    side = 0 if base == base_a else 1
    is_rank = i < 4

    def w2(w):
        g.wait_ge(sem["rs%d" % w], (3 if is_rank else 4) * W1E)
        g.remote_dma_fused([RemoteDMATransfer(
            dst_ids=[did(relay_of(w, i))], dma_engine_mask=0x00FF, remote_sem=sem["rl%d" % (w // 2)],
            srcs=[T.xs[8 * w + i] if r == i else T.land[4 * w + r] for r in range(4)],
            dsts=[T.land[2 * (w // 2) + side]], alu_op=1)], local_sem=sem.sent)

    if is_rank:
        g.sync.dma_start(T.xs[0:NP // 2], T.x[0:64, :]).then_inc(sem.ld0, 16)
        g.scalar.dma_start(T.xs[NP // 2:NP], T.x[64:128, :]).then_inc(sem.ld1, 16)
        emask = (1 << W1E) - 1
        for c in range(2):
            g.wait_ge((sem.ld0, sem.ld1)[c], 16)
            todo = [(w, k) for w in range(WPC * c, WPC * (c + 1)) for k in range(8) if k != i]
            g.remote_dma_fused([RemoteDMATransfer(
                dst_ids=[did(base + k)], dma_engine_mask=emask << (W1E * n), remote_sem=sem["rs%d" % w],
                srcs=[T.xs[8 * w + k]], dsts=[T.land[4 * w + i]], alu_op=0)
                for n, (w, k) in enumerate(todo)], local_sem=sem.sent)
        for w in range(NW):
            w2(w)
        for w in range(NW):
            q = g.sync if w % 2 == 0 else g.scalar
            q.wait_ge(sem["farr%d" % w], 64)
            q.dma_start(T.y[XR * w:XR * (w + 1), :], T.fin[8 * w:8 * (w + 1)]).then_inc(sem["st%d" % w], 16)
        for w in range(NW):
            q = g.sync if w % 2 == 0 else g.scalar
            q.wait_ge(sem["st%d" % w], 16)
        g.wait_ge(sem.sent, (7 * W1E + 8) * NW)
    else:
        j = i - 4
        g.vector.memset(T.zs[:], 0.0).then_inc(sem.zm, 1)
        g.sync.wait_ge(sem.zm, 1)
        g.sync.dma_start(T.zd[:], T.zs[:]).then_inc(sem.zr, 16)
        for w in range(NW):
            w2(w)
        g.wait_ge(sem.zr, 16)
        ranks = [base + r for r in range(4)]
        for w in range(NW):
            g.wait_ge(sem["harr%d" % w], 16)
            g.remote_dma_fused([RemoteDMATransfer(
                dst_ids=[did(r) for r in ranks], dma_engine_mask=0xFF << (8 * h), remote_sem=sem["farr%d" % w],
                srcs=[T.hs[2 * w + h], T.zd[:]], dsts=[T.fin[8 * w + 2 * j + h]] * 4, alu_op=2) for h in range(2)],
                local_sem=sem.sent)
        g.wait_ge(sem.sent, (8 + 16) * NW)
